import numpy as np
import ml_dtypes


def mxq(x, axis, fmt="e4m3"):
    dtype, down = {"e4m3": (ml_dtypes.float8_e4m3fn, 7), "e5m2": (ml_dtypes.float8_e5m2, 14)}[fmt]
    v = np.moveaxis(np.asarray(x, np.float32).astype(ml_dtypes.bfloat16).astype(np.float64), axis, -1)
    blocks = v.reshape(v.shape[:-1] + (-1, 32))
    amax = np.abs(blocks).max(-1, keepdims=True)
    byte = np.maximum(np.where(amax > 0, np.frexp(amax)[1] - 1 + 127, 0) - down, 1)
    scale = np.exp2(byte - 127.0)
    codes = (blocks / scale).astype(np.float32).astype(dtype).astype(np.float64)
    return np.moveaxis((codes * scale).reshape(v.shape), -1, axis)


WIDE = False


def mx_kscale(k):
    if not WIDE:
        return np.ones(k)
    levels = np.array([10, -10, 5, -5, 0])
    if k % 512:
        return np.exp2(np.random.permutation(np.resize(levels, k // 32))).repeat(32)
    a = np.empty((k // 512, 16))
    for p in range(k // 512):
        a[p, :8] = np.random.permutation(np.resize(levels, 8))
        for g in range(8):
            far = levels[np.abs(levels - a[p, g]) >= 10]
            a[p, g + 8] = far[np.random.randint(len(far))]
    return np.exp2(a.ravel()).repeat(32)


def f64(x):
    return np.asarray(x).astype(np.float64)


def striped(idx):
    return np.tile(idx.reshape(-1, 16).T, (8, 1)).astype(np.uint16)


def unstriped(offs):
    return offs[:16].T.reshape(-1).astype(np.int64)


E2M1 = np.array([0.0, 0.5, 1.0, 1.5, 2.0, 3.0, 4.0, 6.0, -0.0, -0.5, -1.0, -1.5, -2.0, -3.0, -4.0, -6.0])


def pack_weight(w, fmt):
    k, n = w.shape
    w = f64(np.asarray(w, np.float32).astype(ml_dtypes.bfloat16)).reshape(k // 32, 32, n)
    amax = np.abs(w).max(1)
    if fmt == "e4m3":
        byte = np.frexp(amax)[1] - 1 + 127 - 7
    else:
        mant, ex = np.frexp(amax / 6.0)
        byte = np.where(mant > 0.5, ex, ex - 1) + 127
    byte = np.clip(np.where(amax > 0, byte, 1), 1, 254)
    scaled = (w * np.exp2(127.0 - byte)[:, None, :]).reshape(k, n).astype(np.float32)
    by_word = np.ascontiguousarray(scaled.reshape(k // 512, 128, 4, n).transpose(0, 1, 3, 2))
    if fmt == "e4m3":
        words = by_word.astype(ml_dtypes.float8_e4m3fn).view(np.uint8)
    else:
        c = by_word.astype(ml_dtypes.float4_e2m1fn).view(np.uint8) & 0xF
        words = (c[..., 0::2] | (c[..., 1::2] << 4)).reshape(k // 512, 128, 2 * n)
    return np.ascontiguousarray(words), np.ascontiguousarray(byte.astype(np.uint8).reshape(k // 512, 16, n))


def unpack_weight(words, scales, fmt):
    g, _, n = scales.shape
    words = np.ascontiguousarray(words).reshape(g, 128, n, -1)
    if fmt == "e4m3":
        vals = words.view(ml_dtypes.float8_e4m3fn).astype(np.float64)
    else:
        nib = np.empty((g, 128, n, 4), np.uint8)
        nib[..., 0::2] = words & 0xF
        nib[..., 1::2] = words >> 4
        vals = E2M1[nib]
    vals = vals * np.repeat(np.exp2(scales.astype(np.float64) - 127.0), 8, axis=1)[..., None]
    return vals.transpose(0, 1, 3, 2).reshape(g * 512, n)


def gelu(v):
    return 0.5 * v * (1.0 + np.tanh(np.sqrt(2.0 / np.pi) * (v + 0.044715 * v**3)))


def twice(P):
    return np.random.permutation(np.repeat(np.arange(P), 2))


def bf(x):
    return np.asarray(x, np.float32).astype(ml_dtypes.bfloat16)


def planes(Y):
    n, m = Y.shape
    b = f64(bf(Y)).reshape(n // 32, 32, m)
    amax = np.abs(b).max(1)
    byte = np.clip(np.where(amax > 0, np.frexp(amax)[1] - 1 + 127 - 7, 1), 1, 254)
    codes = (b * np.exp2(127.0 - byte)[:, None, :]).reshape(n, m).astype(np.float32).astype(ml_dtypes.float8_e4m3fn).view(np.uint8)
    words = codes.reshape(n // 512, 128, 4, m).transpose(0, 1, 3, 2)
    return np.ascontiguousarray(words), np.ascontiguousarray(byte.astype(np.uint8).reshape(n // 512, 16, m))


K, H, T, S, P = 1024, 1024, 4096, 1024, 512

def setup_inputs():
    n = np.random.standard_normal
    s = mx_kscale(K)[:, None]
    u = mx_kscale(H)[:, None]
    d = {}
    d["tab_words"], d["tab_scales"] = pack_weight(n((K, T)) * s, "e4m3")
    d["offs"] = striped(np.random.permutation(T)[:S])
    d["pos1"] = striped(np.random.permutation(S)[:P])
    d["pos2"] = striped(np.random.permutation(S)[:P])
    d["pos3"] = striped(twice(P))
    d["w1"] = (1.4 * n((K, H)) / K ** 0.5 / s).astype(np.float32)
    d["w2_words"], d["w2_scales"] = pack_weight(0.8 * n((K, H)) / K ** 0.5 / s * u.T, "e2m1")
    d["gv"] = (np.exp(0.3 * n(H)) * u[:, 0]).astype(np.float32)
    d["w3"] = (n((H, H)) / H ** 0.5 / u).astype(np.float32)
    d["hs"] = (np.exp(0.3 * n(H)) / u[:, 0]).astype(np.float32)
    d["blend"] = (np.exp(0.8 * n((H, 1))) * np.exp(0.4 * n((H, S)))).astype(np.float32)
    return d

def reference(tab_words, tab_scales, offs, pos1, pos2, pos3, w1, w2_words, w2_scales, gv, w3, hs, blend):
    v = unpack_weight(tab_words, tab_scales, "e4m3")[:, unstriped(offs)]
    w2 = unpack_weight(w2_words, w2_scales, "e2m1")
    pre = mxq(f64(w1), 0, "e4m3").T @ v
    bent = 0.5 * pre * (1.0 + np.tanh(0.7978845608 * (pre + 0.044715 * pre ** 3)))
    h = f64(gv)[:, None] * bent + (w2.T @ v)
    z = np.maximum(h[:, unstriped(pos1)], h[:, unstriped(pos2)])
    seam = mxq(f64(w3), 0, "e4m3").T @ mxq(z, 0, "e4m3")
    y = f64(blend) * (seam[:, unstriped(pos3)] + f64(hs)[:, None] * h)
    words, scales = planes(y)
    return y, words, scales

@@ -1,0 +1,271 @@
+from contextlib import ExitStack
+
+import concourse.mybir as mybir
+
+K, H, T, S, M = 1024, 1024, 4096, 1024, 512
+FLOPS = 2 * (2 * K * H * S + H * H * M)
+
+F32 = mybir.dt.float32
+BF16 = mybir.dt.bfloat16
+I32 = mybir.dt.int32
+U32 = mybir.dt.uint32
+U16 = mybir.dt.uint16
+U8 = mybir.dt.uint8
+FP8X4 = mybir.dt.float8_e4m3fn_x4
+FP4X4 = mybir.dt.float4_e2m1fn_x4
+ALU = mybir.AluOpType
+ACT = mybir.ActivationFunctionType
+
+P = 128
+PACK = 4
+GROUP = P * PACK
+BANK = 512
+SPARE = 32
+VECTOR_SHARE = 96
+CHUNKS = [(0, 0, 512), (0, 512, 512), (1, 0, 512), (1, 512, 256), (1, 768, 256)]
+
+
+def tile_list_dome_seam_encoder_kernel(
+    tc, tab_words, tab_scales, offs, pos1, pos2, pos3, w1, w2_words, w2_scales, gv, w3, hs, blend,
+    out_0, out_1, out_2,
+):
+    nc = tc.nc
+    with ExitStack() as ctx:
+        keep = ctx.enter_context(tc.tile_pool(name="keep", bufs=1))
+        ring = ctx.enter_context(tc.tile_pool(name="ring", bufs=3))
+        psum = ctx.enter_context(tc.psum_pool(name="psum", bufs=4))
+
+        def kept(shape, dtype, name):
+            return keep.tile(shape, dtype, name=name, align_bytes=64)
+
+        def load_list(src, name):
+            tile = keep.tile([P, src.shape[1]], U16, name=name)
+            nc.sync.dma_start(tile[:], src)
+            return tile
+
+        def load_rows(src, g, c):
+            raw = ring.tile([P, PACK, BANK], F32, name="raw", bufs=6, align_bytes=64)
+            rows = src[GROUP * g : GROUP * (g + 1), BANK * c : BANK * (c + 1)]
+            nc.sync.dma_start(raw[:], rows.rearrange("(p i) c -> p i c", i=PACK))
+            return raw
+
+        def new_stage():
+            return ring.tile([P, PACK * BANK], BF16, name="stage", align_bytes=64)
+
+        tab_sc = kept([P, T], U8, "tab_sc")
+        w2_sc_raw = kept([P, 2 * H], U8, "w2_sc_raw")
+        v_sc = kept([P, 2 * S], U8, "v_sc")
+        for tile in (tab_sc, w2_sc_raw, v_sc):
+            nc.vector.memset(tile[:].bitcast(I32), 0)
+        seam = [kept([P, M + SPARE], F32, "seam%d" % n) for n in range(8)]
+        for tile in seam:
+            nc.vector.memset(tile[:, M:], 0.0)
+
+        nc.gpsimd.dma_start(
+            tab_sc[0:P:4, :].bitcast(I32), tab_scales.rearrange("a q t -> (a q) t").bitcast(I32)
+        )
+        for q in range(4):
+            nc.gpsimd.dma_start(
+                w2_sc_raw[32 * q : 32 * q + 4, :].bitcast(I32).rearrange("r (a c) -> r a c", a=2),
+                w2_scales[:, 4 * q : 4 * q + 4, :].bitcast(I32).rearrange("a r c -> r a c"),
+            )
+        def load_vector(src, name):
+            tile = kept([P, 2 * PACK], F32, name)
+            nc.sync.dma_start(
+                tile[:].rearrange("p (g t) -> p g t", g=2), src.rearrange("(g p t) -> p g t", g=2, t=PACK)
+            )
+            return tile
+
+        idx = load_list(offs, "idx")
+        gain = load_vector(gv, "gain")
+        w2_raw = kept([P, 2 * 2 * H], U8, "w2_raw")
+        nc.sync.dma_start(
+            w2_raw[:].bitcast(I32).rearrange("p (a c) -> p a c", a=2),
+            w2_words.bitcast(I32).rearrange("a p c -> p a c"),
+        )
+        tab = [kept([P, T], U32, "tab%d" % a) for a in range(2)]
+        for a in range(2):
+            nc.sync.dma_start(
+                tab[a][:].bitcast(I32), tab_words[a].rearrange("p t i -> p (t i)").bitcast(I32)
+            )
+        w1_raw = {}
+        for a in range(2):
+            w1_raw[a, 0] = load_rows(w1, a, 0)
+        p1 = load_list(pos1, "p1")
+        p2 = load_list(pos2, "p2")
+        for a in range(2):
+            w1_raw[a, 1] = load_rows(w1, a, 1)
+        own = load_vector(hs, "own")
+        p3 = load_list(pos3, "p3")
+        w3_raw = {}
+        for g in range(2):
+            for b in range(2):
+                w3_raw[b, g] = load_rows(w3, b, g)
+        blend_raw = {}
+        for g in range(2):
+            for c in range(2):
+                blend_raw[g, c] = load_rows(blend, g, c)
+
+        w2_codes = kept([P, 2 * 2 * H], U8, "w2_codes")
+        nc.vector.tensor_copy(
+            w2_codes[:].bitcast(U16).rearrange("p (g t m) -> p g t m", g=4, t=PACK),
+            w2_raw[:].bitcast(U16).rearrange("p (g m t) -> p g t m", g=4, t=PACK),
+        )
+        picked_sc = kept([P, S], U8, "picked_sc")
+        nc.vector.tensor_copy(picked_sc[:], tab_sc[:].indirect(idx[:]))
+        for a in range(2):
+            for q in range(4):
+                first = 64 * a + 16 * q
+                nc.gpsimd.dma_start(
+                    v_sc[32 * q : 32 * q + 4, S * a : S * (a + 1)].bitcast(I32),
+                    picked_sc[first : first + 16 : 4, :].bitcast(I32),
+                )
+        w2_sc = kept([P, 2 * H], U8, "w2_sc")
+        nc.vector.tensor_copy(
+            w2_sc[:].rearrange("p (g t m) -> p g t m", g=4, t=PACK),
+            w2_sc_raw[:].rearrange("p (g m t) -> p g t m", g=4, t=PACK),
+        )
+        v_codes = [kept([P, S], U32, "v_codes%d" % a) for a in range(2)]
+        for a in range(2):
+            nc.vector.tensor_copy(v_codes[a][:], tab[a][:].indirect(idx[:]))
+
+        def deal_views(stage, raw, lo, hi):
+            dst = stage[:].rearrange("p (t m i) -> p m i t", t=PACK, i=PACK)[:, lo:hi]
+            src = raw[:].rearrange("p i (m t) -> p m i t", t=PACK)[:, lo:hi]
+            return dst, src
+
+        def round_weight(raw, vector_share=0):
+            stage = new_stage()
+            if vector_share:
+                nc.vector.tensor_copy(*deal_views(stage, raw, 0, vector_share))
+            nc.scalar.copy(*deal_views(stage, raw, vector_share, P))
+            return stage
+
+        def quantise(stage, width, name):
+            codes = kept([P, width], U32, name + "_codes")
+            scales = kept([P, width], U8, name + "_sc")
+            nc.vector.quantize_mx(codes[:].bitcast(FP8X4), scales[:], stage[:, : PACK * width])
+            return codes, scales
+
+        w1_mx, w3_mx, z_mx, staged = {}, {}, {}, {}
+        w1_mx[0, 0] = quantise(round_weight(w1_raw[0, 0]), BANK, "w1_00")
+        w1_mx[1, 0] = quantise(round_weight(w1_raw[1, 0], VECTOR_SHARE), BANK, "w1_10")
+
+        h = [kept([P, S], F32, "h%d" % n) for n in range(8)]
+
+        def first_stage(b, t):
+            n = PACK * b + t
+            for c in range(2):
+                cols = slice(BANK * c, BANK * (c + 1))
+                pre = psum.tile([P, BANK], F32, name="pre")
+                straight = psum.tile([P, BANK], F32, name="straight")
+                for a in range(2):
+                    codes, scales = w1_mx[a, b]
+                    nc.tensor.matmul_mx(
+                        pre[:], lhsT=codes[:, P * t : P * (t + 1)].bitcast(FP8X4), lhsT_scale=scales[:, P * t : P * (t + 1)],
+                        rhs=v_codes[a][:, cols].bitcast(FP8X4), rhs_scale=v_sc[:, S * a + BANK * c : S * a + BANK * (c + 1)],
+                        start=(a == 0), stop=(a == 1),
+                    )
+                for a in range(2):
+                    col = H * a + P * n
+                    nc.tensor.matmul_mx(
+                        straight[:], lhsT=w2_codes[:, 2 * col : 2 * (col + P)].bitcast(FP4X4), lhsT_scale=w2_sc[:, col : col + P],
+                        rhs=v_codes[a][:, cols].bitcast(FP8X4), rhs_scale=v_sc[:, S * a + BANK * c : S * a + BANK * (c + 1)],
+                        start=(a == 0), stop=(a == 1),
+                    )
+                bent = ring.tile([P, BANK], F32, name="bent")
+                nc.scalar.activation(bent[:], pre[:], ACT.Gelu_apprx_tanh)
+                nc.vector.scalar_tensor_tensor(h[n][:, cols], bent[:], gain[:, n : n + 1], straight[:], ALU.mult, ALU.add)
+
+        def new_quad():
+            return ring.tile([P, PACK, BANK], F32, name="quad", align_bytes=64)
+
+        def woven(stage, width):
+            return stage[:, : PACK * width].rearrange("p (c i t) -> p c t i", i=2, t=PACK)
+
+        def paired(quad, lo, width):
+            return quad[:, :, lo : lo + width].rearrange("p t (c i) -> p c t i", i=2)
+
+        def scale_own(n):
+            nc.scalar.activation(h[n][:], h[n][:], ACT.Copy, scale=own[:, n : n + 1])
+
+        for b in range(2):
+            left, right = new_quad(), new_quad()
+            for t in range(PACK):
+                n = PACK * b + t
+                first_stage(b, t)
+                nc.vector.tensor_copy(left[:, t, :], h[n][:].indirect(p1[:]))
+                nc.vector.tensor_copy(right[:, t, :], h[n][:].indirect(p2[:]))
+                if n in (0, 1):
+                    staged[n] = round_weight(w1_raw[n, 1])
+                if n in (1, 2):
+                    w1_mx[n - 1, 1] = quantise(staged[n - 1], BANK, "w1_%d1" % (n - 1))
+                if n in (3, 4, 5, 6):
+                    g, bb = divmod(n - 3, 2)
+                    staged[n] = round_weight(w3_raw[bb, g])
+                if n in (4, 5, 6):
+                    g, bb = divmod(n - 4, 2)
+                    w3_mx[bb, g] = quantise(staged[n - 1], BANK, "w3_%d%d" % (bb, g))
+                if n >= 4:
+                    scale_own(n - 4)
+            stage = new_stage()
+            nc.vector.tensor_tensor(woven(stage, M), paired(left, 0, M), paired(right, 0, M), ALU.max)
+            z_mx[b] = quantise(stage, M, "z%d" % b)
+        w3_mx[1, 1] = quantise(staged[6], BANK, "w3_11")
+
+        for g in range(2):
+            for t in range(PACK):
+                acc = psum.tile([P, BANK], F32, name="pre")
+                for b in range(2):
+                    codes, scales = w3_mx[b, g]
+                    nc.tensor.matmul_mx(
+                        acc[:], lhsT=codes[:, P * t : P * (t + 1)].bitcast(FP8X4), lhsT_scale=scales[:, P * t : P * (t + 1)],
+                        rhs=z_mx[b][0][:].bitcast(FP8X4), rhs_scale=z_mx[b][1][:],
+                        start=(b == 0), stop=(b == 1),
+                    )
+                nc.scalar.copy(seam[PACK * g + t][:, :M], acc[:])
+        for t in range(PACK):
+            scale_own(PACK + t)
+
+        y_sc = [kept([P, S], U8, "y_sc%d" % g) for g in range(2)]
+        rounded = {}
+
+        def combine(k):
+            g, lo, width = CHUNKS[k]
+            total = new_quad()
+            for t in range(PACK):
+                n = PACK * g + t
+                nc.vector.tensor_tensor(
+                    total[:, t, :width], seam[n][:].indirect(p3[:, lo // 16 : (lo + width) // 16]),
+                    h[n][:, lo : lo + width], ALU.add,
+                )
+            y = blend_raw[g, lo // BANK]
+            cols = slice(lo % BANK, lo % BANK + width)
+            nc.vector.tensor_tensor(y[:, :, cols], total[:, :, :width], y[:, :, cols], ALU.mult)
+            rows = out_0[GROUP * g : GROUP * (g + 1), lo : lo + width]
+            nc.sync.dma_start(rows.rearrange("(p t) j -> p t j", t=PACK), y[:, :, cols])
+            stage = new_stage()
+            if k == len(CHUNKS) - 1:
+                nc.vector.tensor_copy(woven(stage, width), paired(y, lo % BANK, width))
+            else:
+                nc.scalar.copy(woven(stage, width), paired(y, lo % BANK, width))
+            rounded[k] = stage
+
+        def planes(k):
+            g, lo, width = CHUNKS[k]
+            codes = kept([P, width], U32, "y_codes%d" % k)
+            nc.vector.quantize_mx(codes[:].bitcast(FP8X4), y_sc[g][:, lo : lo + width], rounded[k][:, : PACK * width])
+            words = out_1[g].rearrange("p m t -> p (m t)")[:, PACK * lo : PACK * (lo + width)]
+            nc.sync.dma_start(words.bitcast(I32), codes[:].bitcast(I32))
+            if lo + width == S:
+                for q in range(4):
+                    queue = nc.scalar if g == 1 and q % 2 else nc.sync
+                    queue.dma_start(
+                        out_2[g, 4 * q : 4 * q + 4, :].bitcast(I32), y_sc[g][32 * q : 32 * q + 4, :].bitcast(I32)
+                    )
+
+        for k in range(len(CHUNKS)):
+            combine(k)
+            if k:
+                planes(k - 1)
+        planes(len(CHUNKS) - 1)

@@ -21,7 +21,7 @@ PACK = 4
 GROUP = P * PACK
 BANK = 512
 SPARE = 32
-VECTOR_SHARE = 96
+ON_GPSIMD = ()
 CHUNKS = [(0, 0, 512), (0, 512, 512), (1, 0, 512), (1, 512, 256), (1, 768, 256)]
 
 
@@ -44,7 +44,7 @@ def tile_list_dome_seam_encoder_kernel(
             return tile
 
         def load_rows(src, g, c):
-            raw = ring.tile([P, PACK, BANK], F32, name="raw", bufs=6, align_bytes=64)
+            raw = ring.tile([P, PACK, BANK], F32, name="raw", bufs=4, align_bytes=64)
             rows = src[GROUP * g : GROUP * (g + 1), BANK * c : BANK * (c + 1)]
             nc.sync.dma_start(raw[:], rows.rearrange("(p i) c -> p i c", i=PACK))
             return raw
@@ -52,18 +52,19 @@ def tile_list_dome_seam_encoder_kernel(
         def new_stage():
             return ring.tile([P, PACK * BANK], BF16, name="stage", align_bytes=64)
 
-        tab_sc = kept([P, T], U8, "tab_sc")
+        tab_sc = ring.tile([P, T], U8, name="raw", bufs=4, align_bytes=64)
+        picked_sc = kept([P, S], U8, "picked_sc")
         w2_sc_raw = kept([P, 2 * H], U8, "w2_sc_raw")
         v_sc = kept([P, 2 * S], U8, "v_sc")
-        for tile in (tab_sc, w2_sc_raw, v_sc):
-            nc.vector.memset(tile[:].bitcast(I32), 0)
+        nc.vector.memset(w2_sc_raw[:].bitcast(I32), 0)
+        for q in range(4):
+            nc.vector.memset(tab_sc[32 * q : 32 * q + 24, :].bitcast(I32), 0)
+        nc.vector.memset(v_sc[:].bitcast(I32), 0)
         seam = [kept([P, M + SPARE], F32, "seam%d" % n) for n in range(8)]
-        for tile in seam:
+        for tile in seam[1:]:
             nc.vector.memset(tile[:, M:], 0.0)
+        nc.scalar.activation(seam[0][:, M:], seam[1][:, M:], ACT.Gelu_apprx_tanh)
 
-        nc.gpsimd.dma_start(
-            tab_sc[0:P:4, :].bitcast(I32), tab_scales.rearrange("a q t -> (a q) t").bitcast(I32)
-        )
         for q in range(4):
             nc.gpsimd.dma_start(
                 w2_sc_raw[32 * q : 32 * q + 4, :].bitcast(I32).rearrange("r (a c) -> r a c", a=2),
@@ -76,27 +77,41 @@ def tile_list_dome_seam_encoder_kernel(
             )
             return tile
 
+        def load_table(a):
+            tile = kept([P, T], U32, "tab%d" % a)
+            nc.sync.dma_start(tile[:].bitcast(I32), tab_words[a].rearrange("p t i -> p (t i)").bitcast(I32))
+            return tile
+
         idx = load_list(offs, "idx")
-        gain = load_vector(gv, "gain")
-        w2_raw = kept([P, 2 * 2 * H], U8, "w2_raw")
+        for q in range(4):
+            nc.sync.dma_start(
+                tab_sc[32 * q + 24 : 32 * q + 32, :].bitcast(I32), tab_scales[:, 4 * q : 4 * q + 4, :].bitcast(I32)
+            )
+        tab = [load_table(0)]
+        p1 = load_list(pos1, "p1")
+        p2 = load_list(pos2, "p2")
+        w2_raw = ring.tile([P, 2 * 2 * H], U8, name="raw", bufs=4, align_bytes=64)
         nc.sync.dma_start(
             w2_raw[:].bitcast(I32).rearrange("p (a c) -> p a c", a=2),
             w2_words.bitcast(I32).rearrange("a p c -> p a c"),
         )
-        tab = [kept([P, T], U32, "tab%d" % a) for a in range(2)]
-        for a in range(2):
-            nc.sync.dma_start(
-                tab[a][:].bitcast(I32), tab_words[a].rearrange("p t i -> p (t i)").bitcast(I32)
-            )
         w1_raw = {}
         for a in range(2):
             w1_raw[a, 0] = load_rows(w1, a, 0)
-        p1 = load_list(pos1, "p1")
-        p2 = load_list(pos2, "p2")
+        p3 = load_list(pos3, "p3")
+        gain = load_vector(gv, "gain")
+        tab.append(load_table(1))
+        own = load_vector(hs, "own")
+
+        v_codes = [kept([P, S], U32, "v_codes%d" % a) for a in range(2)]
+        nc.vector.tensor_copy(picked_sc[:], tab_sc[:].indirect(idx[:]))
+        for a in range(2):
+            first = 24 + 4 * a
+            nc.gpsimd.dma_start(
+                v_sc[0:100, S * a : S * (a + 1)].bitcast(I32), picked_sc[first : first + 100, :].bitcast(I32)
+            )
         for a in range(2):
             w1_raw[a, 1] = load_rows(w1, a, 1)
-        own = load_vector(hs, "own")
-        p3 = load_list(pos3, "p3")
         w3_raw = {}
         for g in range(2):
             for b in range(2):
@@ -106,39 +121,24 @@ def tile_list_dome_seam_encoder_kernel(
             for c in range(2):
                 blend_raw[g, c] = load_rows(blend, g, c)
 
+        nc.vector.tensor_copy(v_codes[0][:], tab[0][:].indirect(idx[:]))
         w2_codes = kept([P, 2 * 2 * H], U8, "w2_codes")
         nc.vector.tensor_copy(
             w2_codes[:].bitcast(U16).rearrange("p (g t m) -> p g t m", g=4, t=PACK),
             w2_raw[:].bitcast(U16).rearrange("p (g m t) -> p g t m", g=4, t=PACK),
         )
-        picked_sc = kept([P, S], U8, "picked_sc")
-        nc.vector.tensor_copy(picked_sc[:], tab_sc[:].indirect(idx[:]))
-        for a in range(2):
-            for q in range(4):
-                first = 64 * a + 16 * q
-                nc.gpsimd.dma_start(
-                    v_sc[32 * q : 32 * q + 4, S * a : S * (a + 1)].bitcast(I32),
-                    picked_sc[first : first + 16 : 4, :].bitcast(I32),
-                )
         w2_sc = kept([P, 2 * H], U8, "w2_sc")
         nc.vector.tensor_copy(
             w2_sc[:].rearrange("p (g t m) -> p g t m", g=4, t=PACK),
             w2_sc_raw[:].rearrange("p (g m t) -> p g t m", g=4, t=PACK),
         )
-        v_codes = [kept([P, S], U32, "v_codes%d" % a) for a in range(2)]
-        for a in range(2):
-            nc.vector.tensor_copy(v_codes[a][:], tab[a][:].indirect(idx[:]))
 
-        def deal_views(stage, raw, lo, hi):
-            dst = stage[:].rearrange("p (t m i) -> p m i t", t=PACK, i=PACK)[:, lo:hi]
-            src = raw[:].rearrange("p i (m t) -> p m i t", t=PACK)[:, lo:hi]
-            return dst, src
-
-        def round_weight(raw, vector_share=0):
+        def round_weight(raw):
             stage = new_stage()
-            if vector_share:
-                nc.vector.tensor_copy(*deal_views(stage, raw, 0, vector_share))
-            nc.scalar.copy(*deal_views(stage, raw, vector_share, P))
+            dst = stage[:].rearrange("p (t m i) -> p m i t", t=PACK, i=PACK)
+            src = raw[:].rearrange("p i (m t) -> p m i t", t=PACK)
+            for t in (0, 2):
+                nc.scalar.copy(dst[:, :, :, t : t + 2], src[:, :, :, t : t + 2])
             return stage
 
         def quantise(stage, width, name):
@@ -149,12 +149,14 @@ def tile_list_dome_seam_encoder_kernel(
 
         w1_mx, w3_mx, z_mx, staged = {}, {}, {}, {}
         w1_mx[0, 0] = quantise(round_weight(w1_raw[0, 0]), BANK, "w1_00")
-        w1_mx[1, 0] = quantise(round_weight(w1_raw[1, 0], VECTOR_SHARE), BANK, "w1_10")
+        w1_mx[1, 0] = quantise(round_weight(w1_raw[1, 0]), BANK, "w1_10")
+        nc.vector.tensor_copy(v_codes[1][:, :BANK], tab[1][:].indirect(idx[:, :32]))
+        nc.vector.tensor_copy(v_codes[1][:, BANK:], tab[1][:].indirect(idx[:, 32:]))
 
         h = [kept([P, S], F32, "h%d" % n) for n in range(8)]
 
-        def first_stage(b, t):
-            n = PACK * b + t
+        def first_stage(n, bent):
+            b, t = divmod(n, PACK)
             for c in range(2):
                 cols = slice(BANK * c, BANK * (c + 1))
                 pre = psum.tile([P, BANK], F32, name="pre")
@@ -173,12 +175,16 @@ def tile_list_dome_seam_encoder_kernel(
                         rhs=v_codes[a][:, cols].bitcast(FP8X4), rhs_scale=v_sc[:, S * a + BANK * c : S * a + BANK * (c + 1)],
                         start=(a == 0), stop=(a == 1),
                     )
-                bent = ring.tile([P, BANK], F32, name="bent")
-                nc.scalar.activation(bent[:], pre[:], ACT.Gelu_apprx_tanh)
-                nc.vector.scalar_tensor_tensor(h[n][:, cols], bent[:], gain[:, n : n + 1], straight[:], ALU.mult, ALU.add)
+                nc.scalar.activation(bent[c], pre[:], ACT.Gelu_apprx_tanh)
+                if n in ON_GPSIMD:
+                    nc.scalar.copy(h[n][:, cols], straight[:])
+                    nc.gpsimd.tensor_scalar(bent[c], bent[c], gain[:, n : n + 1], 0.0, ALU.mult, ALU.add)
+                    nc.gpsimd.tensor_tensor(h[n][:, cols], h[n][:, cols], bent[c], ALU.add)
+                else:
+                    nc.vector.scalar_tensor_tensor(h[n][:, cols], bent[c], gain[:, n : n + 1], straight[:], ALU.mult, ALU.add)
 
         def new_quad():
-            return ring.tile([P, PACK, BANK], F32, name="quad", align_bytes=64)
+            return ring.tile([P, PACK, BANK], F32, name="quad", bufs=4, align_bytes=64)
 
         def woven(stage, width):
             return stage[:, : PACK * width].rearrange("p (c i t) -> p c t i", i=2, t=PACK)
@@ -189,29 +195,54 @@ def tile_list_dome_seam_encoder_kernel(
         def scale_own(n):
             nc.scalar.activation(h[n][:], h[n][:], ACT.Copy, scale=own[:, n : n + 1])
 
+        ends = [(new_quad(), new_quad()) for b in range(2)]
+
+        def end_slots(n):
+            b, t = divmod(n, PACK)
+            return ends[b][0][:, t, :], ends[b][1][:, t, :]
+
+        def look_up(n):
+            left, right = end_slots(n)
+            nc.vector.tensor_copy(left, h[n][:].indirect(p1[:]))
+            nc.vector.tensor_copy(right, h[n][:].indirect(p2[:]))
+
+        def larger(b, stage):
+            nc.vector.tensor_tensor(woven(stage, M), paired(ends[b][0], 0, M), paired(ends[b][1], 0, M), ALU.max)
+
+        first_stage(0, end_slots(PACK - 1))
+        for n in range(1, 8):
+            if n in ON_GPSIMD:
+                aside = ring.tile([P, 2, BANK], F32, name="aside", bufs=2)
+                first_stage(n, (aside[:, 0, :], aside[:, 1, :]))
+            else:
+                first_stage(n, end_slots(n - 1))
+            look_up(n - 1)
+            if n in (1, 2):
+                staged[n] = round_weight(w1_raw[n - 1, 1])
+            if n in (2, 3):
+                w1_mx[n - 2, 1] = quantise(staged[n - 1], BANK, "w1_%d1" % (n - 2))
+            if n in (3, 4, 5, 6):
+                g, b = divmod(n - 3, 2)
+                staged[n] = round_weight(w3_raw[b, g])
+            if n == 4:
+                z_stage = new_stage()
+                larger(0, z_stage)
+            if n in (4, 5):
+                w3_mx[n - 4, 0] = quantise(staged[n - 1], BANK, "w3_%d0" % (n - 4))
+            if n == 4:
+                z_mx[0] = quantise(z_stage, M, "z0")
+            if n >= 4:
+                scale_own(n - 4)
+        look_up(7)
+        z_stage = keep.tile([P, PACK * M], BF16, name="late", align_bytes=64)
+        larger(1, z_stage)
+        z_mx[1] = quantise(z_stage, M, "z1")
+        late_codes = keep.tile([P, 2 * BANK], U32, name="late", align_bytes=64)
         for b in range(2):
-            left, right = new_quad(), new_quad()
-            for t in range(PACK):
-                n = PACK * b + t
-                first_stage(b, t)
-                nc.vector.tensor_copy(left[:, t, :], h[n][:].indirect(p1[:]))
-                nc.vector.tensor_copy(right[:, t, :], h[n][:].indirect(p2[:]))
-                if n in (0, 1):
-                    staged[n] = round_weight(w1_raw[n, 1])
-                if n in (1, 2):
-                    w1_mx[n - 1, 1] = quantise(staged[n - 1], BANK, "w1_%d1" % (n - 1))
-                if n in (3, 4, 5, 6):
-                    g, bb = divmod(n - 3, 2)
-                    staged[n] = round_weight(w3_raw[bb, g])
-                if n in (4, 5, 6):
-                    g, bb = divmod(n - 4, 2)
-                    w3_mx[bb, g] = quantise(staged[n - 1], BANK, "w3_%d%d" % (bb, g))
-                if n >= 4:
-                    scale_own(n - 4)
-            stage = new_stage()
-            nc.vector.tensor_tensor(woven(stage, M), paired(left, 0, M), paired(right, 0, M), ALU.max)
-            z_mx[b] = quantise(stage, M, "z%d" % b)
-        w3_mx[1, 1] = quantise(staged[6], BANK, "w3_11")
+            scales = kept([P, BANK], U8, "w3_%d1_sc" % b)
+            codes = late_codes[:, BANK * b : BANK * (b + 1)]
+            nc.vector.quantize_mx(codes.bitcast(FP8X4), scales[:], staged[5 + b][:])
+            w3_mx[b, 1] = codes, scales
 
         for g in range(2):
             for t in range(PACK):
@@ -230,15 +261,21 @@ def tile_list_dome_seam_encoder_kernel(
         y_sc = [kept([P, S], U8, "y_sc%d" % g) for g in range(2)]
         rounded = {}
 
-        def combine(k):
+        totals = {}
+
+        def fetch(k, t):
             g, lo, width = CHUNKS[k]
-            total = new_quad()
-            for t in range(PACK):
-                n = PACK * g + t
-                nc.vector.tensor_tensor(
-                    total[:, t, :width], seam[n][:].indirect(p3[:, lo // 16 : (lo + width) // 16]),
-                    h[n][:, lo : lo + width], ALU.add,
-                )
+            if t == 0:
+                totals[k] = new_quad()
+            n = PACK * g + t
+            nc.vector.tensor_tensor(
+                totals[k][:, t, :width], seam[n][:].indirect(p3[:, lo // 16 : (lo + width) // 16]),
+                h[n][:, lo : lo + width], ALU.add,
+            )
+
+        def finish(k):
+            g, lo, width = CHUNKS[k]
+            total = totals[k]
             y = blend_raw[g, lo // BANK]
             cols = slice(lo % BANK, lo % BANK + width)
             nc.vector.tensor_tensor(y[:, :, cols], total[:, :, :width], y[:, :, cols], ALU.mult)
@@ -265,7 +302,12 @@ def tile_list_dome_seam_encoder_kernel(
                     )
 
         for k in range(len(CHUNKS)):
-            combine(k)
+            fetch(k, 0)
+            if k:
+                finish(k - 1)
+            for t in range(1, PACK):
+                fetch(k, t)
             if k:
                 planes(k - 1)
+        finish(len(CHUNKS) - 1)
         planes(len(CHUNKS) - 1)

from contextlib import ExitStack

import concourse.mybir as mybir

K, H, T, S, M = 1024, 1024, 4096, 1024, 512
FLOPS = 2 * (2 * K * H * S + H * H * M)

F32 = mybir.dt.float32
BF16 = mybir.dt.bfloat16
I32 = mybir.dt.int32
U32 = mybir.dt.uint32
U16 = mybir.dt.uint16
U8 = mybir.dt.uint8
FP8X4 = mybir.dt.float8_e4m3fn_x4
FP4X4 = mybir.dt.float4_e2m1fn_x4
ALU = mybir.AluOpType
ACT = mybir.ActivationFunctionType

P = 128
PACK = 4
GROUP = P * PACK
BANK = 512
SPARE = 32
ON_GPSIMD = ()
CHUNKS = [(0, 0, 512), (0, 512, 512), (1, 0, 512), (1, 512, 256), (1, 768, 256)]


def tile_list_dome_seam_encoder_kernel(
    tc, tab_words, tab_scales, offs, pos1, pos2, pos3, w1, w2_words, w2_scales, gv, w3, hs, blend,
    out_0, out_1, out_2,
):
    nc = tc.nc
    with ExitStack() as ctx:
        keep = ctx.enter_context(tc.tile_pool(name="keep", bufs=1))
        ring = ctx.enter_context(tc.tile_pool(name="ring", bufs=3))
        psum = ctx.enter_context(tc.psum_pool(name="psum", bufs=4))

        def kept(shape, dtype, name):
            return keep.tile(shape, dtype, name=name, align_bytes=64)

        def load_list(src, name):
            tile = keep.tile([P, src.shape[1]], U16, name=name)
            nc.sync.dma_start(tile[:], src)
            return tile

        def load_rows(src, g, c):
            raw = ring.tile([P, PACK, BANK], F32, name="raw", bufs=4, align_bytes=64)
            rows = src[GROUP * g : GROUP * (g + 1), BANK * c : BANK * (c + 1)]
            nc.sync.dma_start(raw[:], rows.rearrange("(p i) c -> p i c", i=PACK))
            return raw

        def new_stage():
            return ring.tile([P, PACK * BANK], BF16, name="stage", align_bytes=64)

        tab_sc = ring.tile([P, T], U8, name="raw", bufs=4, align_bytes=64)
        picked_sc = kept([P, S], U8, "picked_sc")
        w2_sc_raw = kept([P, 2 * H], U8, "w2_sc_raw")
        v_sc = kept([P, 2 * S], U8, "v_sc")
        nc.vector.memset(w2_sc_raw[:].bitcast(I32), 0)
        for q in range(4):
            nc.vector.memset(tab_sc[32 * q : 32 * q + 24, :].bitcast(I32), 0)
        nc.vector.memset(v_sc[:].bitcast(I32), 0)
        seam = [kept([P, M + SPARE], F32, "seam%d" % n) for n in range(8)]
        for tile in seam[1:]:
            nc.vector.memset(tile[:, M:], 0.0)
        nc.scalar.activation(seam[0][:, M:], seam[1][:, M:], ACT.Gelu_apprx_tanh)

        for q in range(4):
            nc.gpsimd.dma_start(
                w2_sc_raw[32 * q : 32 * q + 4, :].bitcast(I32).rearrange("r (a c) -> r a c", a=2),
                w2_scales[:, 4 * q : 4 * q + 4, :].bitcast(I32).rearrange("a r c -> r a c"),
            )
        def load_vector(src, name):
            tile = kept([P, 2 * PACK], F32, name)
            nc.sync.dma_start(
                tile[:].rearrange("p (g t) -> p g t", g=2), src.rearrange("(g p t) -> p g t", g=2, t=PACK)
            )
            return tile

        def load_table(a):
            tile = kept([P, T], U32, "tab%d" % a)
            nc.sync.dma_start(tile[:].bitcast(I32), tab_words[a].rearrange("p t i -> p (t i)").bitcast(I32))
            return tile

        idx = load_list(offs, "idx")
        for q in range(4):
            nc.sync.dma_start(
                tab_sc[32 * q + 24 : 32 * q + 32, :].bitcast(I32), tab_scales[:, 4 * q : 4 * q + 4, :].bitcast(I32)
            )
        tab = [load_table(0)]
        p1 = load_list(pos1, "p1")
        p2 = load_list(pos2, "p2")
        w2_raw = ring.tile([P, 2 * 2 * H], U8, name="raw", bufs=4, align_bytes=64)
        nc.sync.dma_start(
            w2_raw[:].bitcast(I32).rearrange("p (a c) -> p a c", a=2),
            w2_words.bitcast(I32).rearrange("a p c -> p a c"),
        )
        w1_raw = {}
        for a in range(2):
            w1_raw[a, 0] = load_rows(w1, a, 0)
        p3 = load_list(pos3, "p3")
        gain = load_vector(gv, "gain")
        tab.append(load_table(1))
        own = load_vector(hs, "own")

        v_codes = [kept([P, S], U32, "v_codes%d" % a) for a in range(2)]
        nc.vector.tensor_copy(picked_sc[:], tab_sc[:].indirect(idx[:]))
        for a in range(2):
            first = 24 + 4 * a
            nc.gpsimd.dma_start(
                v_sc[0:100, S * a : S * (a + 1)].bitcast(I32), picked_sc[first : first + 100, :].bitcast(I32)
            )
        for a in range(2):
            w1_raw[a, 1] = load_rows(w1, a, 1)
        w3_raw = {}
        for g in range(2):
            for b in range(2):
                w3_raw[b, g] = load_rows(w3, b, g)
        blend_raw = {}
        for g in range(2):
            for c in range(2):
                blend_raw[g, c] = load_rows(blend, g, c)

        nc.vector.tensor_copy(v_codes[0][:], tab[0][:].indirect(idx[:]))
        w2_codes = kept([P, 2 * 2 * H], U8, "w2_codes")
        nc.vector.tensor_copy(
            w2_codes[:].bitcast(U16).rearrange("p (g t m) -> p g t m", g=4, t=PACK),
            w2_raw[:].bitcast(U16).rearrange("p (g m t) -> p g t m", g=4, t=PACK),
        )
        w2_sc = kept([P, 2 * H], U8, "w2_sc")
        nc.vector.tensor_copy(
            w2_sc[:].rearrange("p (g t m) -> p g t m", g=4, t=PACK),
            w2_sc_raw[:].rearrange("p (g m t) -> p g t m", g=4, t=PACK),
        )

        def round_weight(raw):
            stage = new_stage()
            dst = stage[:].rearrange("p (t m i) -> p m i t", t=PACK, i=PACK)
            src = raw[:].rearrange("p i (m t) -> p m i t", t=PACK)
            for t in (0, 2):
                nc.scalar.copy(dst[:, :, :, t : t + 2], src[:, :, :, t : t + 2])
            return stage

        def quantise(stage, width, name):
            codes = kept([P, width], U32, name + "_codes")
            scales = kept([P, width], U8, name + "_sc")
            nc.vector.quantize_mx(codes[:].bitcast(FP8X4), scales[:], stage[:, : PACK * width])
            return codes, scales

        w1_mx, w3_mx, z_mx, staged = {}, {}, {}, {}
        w1_mx[0, 0] = quantise(round_weight(w1_raw[0, 0]), BANK, "w1_00")
        w1_mx[1, 0] = quantise(round_weight(w1_raw[1, 0]), BANK, "w1_10")
        nc.vector.tensor_copy(v_codes[1][:, :BANK], tab[1][:].indirect(idx[:, :32]))
        nc.vector.tensor_copy(v_codes[1][:, BANK:], tab[1][:].indirect(idx[:, 32:]))

        h = [kept([P, S], F32, "h%d" % n) for n in range(8)]

        def first_stage(n, bent):
            b, t = divmod(n, PACK)
            for c in range(2):
                cols = slice(BANK * c, BANK * (c + 1))
                pre = psum.tile([P, BANK], F32, name="pre")
                straight = psum.tile([P, BANK], F32, name="straight")
                for a in range(2):
                    codes, scales = w1_mx[a, b]
                    nc.tensor.matmul_mx(
                        pre[:], lhsT=codes[:, P * t : P * (t + 1)].bitcast(FP8X4), lhsT_scale=scales[:, P * t : P * (t + 1)],
                        rhs=v_codes[a][:, cols].bitcast(FP8X4), rhs_scale=v_sc[:, S * a + BANK * c : S * a + BANK * (c + 1)],
                        start=(a == 0), stop=(a == 1),
                    )
                for a in range(2):
                    col = H * a + P * n
                    nc.tensor.matmul_mx(
                        straight[:], lhsT=w2_codes[:, 2 * col : 2 * (col + P)].bitcast(FP4X4), lhsT_scale=w2_sc[:, col : col + P],
                        rhs=v_codes[a][:, cols].bitcast(FP8X4), rhs_scale=v_sc[:, S * a + BANK * c : S * a + BANK * (c + 1)],
                        start=(a == 0), stop=(a == 1),
                    )
                nc.scalar.activation(bent[c], pre[:], ACT.Gelu_apprx_tanh)
                if n in ON_GPSIMD:
                    nc.scalar.copy(h[n][:, cols], straight[:])
                    nc.gpsimd.tensor_scalar(bent[c], bent[c], gain[:, n : n + 1], 0.0, ALU.mult, ALU.add)
                    nc.gpsimd.tensor_tensor(h[n][:, cols], h[n][:, cols], bent[c], ALU.add)
                else:
                    nc.vector.scalar_tensor_tensor(h[n][:, cols], bent[c], gain[:, n : n + 1], straight[:], ALU.mult, ALU.add)

        def new_quad():
            return ring.tile([P, PACK, BANK], F32, name="quad", bufs=4, align_bytes=64)

        def woven(stage, width):
            return stage[:, : PACK * width].rearrange("p (c i t) -> p c t i", i=2, t=PACK)

        def paired(quad, lo, width):
            return quad[:, :, lo : lo + width].rearrange("p t (c i) -> p c t i", i=2)

        def scale_own(n):
            nc.scalar.activation(h[n][:], h[n][:], ACT.Copy, scale=own[:, n : n + 1])

        ends = [(new_quad(), new_quad()) for b in range(2)]

        def end_slots(n):
            b, t = divmod(n, PACK)
            return ends[b][0][:, t, :], ends[b][1][:, t, :]

        def look_up(n):
            left, right = end_slots(n)
            nc.vector.tensor_copy(left, h[n][:].indirect(p1[:]))
            nc.vector.tensor_copy(right, h[n][:].indirect(p2[:]))

        def larger(b, stage):
            nc.vector.tensor_tensor(woven(stage, M), paired(ends[b][0], 0, M), paired(ends[b][1], 0, M), ALU.max)

        first_stage(0, end_slots(PACK - 1))
        for n in range(1, 8):
            if n in ON_GPSIMD:
                aside = ring.tile([P, 2, BANK], F32, name="aside", bufs=2)
                first_stage(n, (aside[:, 0, :], aside[:, 1, :]))
            else:
                first_stage(n, end_slots(n - 1))
            look_up(n - 1)
            if n in (1, 2):
                staged[n] = round_weight(w1_raw[n - 1, 1])
            if n in (2, 3):
                w1_mx[n - 2, 1] = quantise(staged[n - 1], BANK, "w1_%d1" % (n - 2))
            if n in (3, 4, 5, 6):
                g, b = divmod(n - 3, 2)
                staged[n] = round_weight(w3_raw[b, g])
            if n == 4:
                z_stage = new_stage()
                larger(0, z_stage)
            if n in (4, 5):
                w3_mx[n - 4, 0] = quantise(staged[n - 1], BANK, "w3_%d0" % (n - 4))
            if n == 4:
                z_mx[0] = quantise(z_stage, M, "z0")
            if n >= 4:
                scale_own(n - 4)
        look_up(7)
        z_stage = keep.tile([P, PACK * M], BF16, name="late", align_bytes=64)
        larger(1, z_stage)
        z_mx[1] = quantise(z_stage, M, "z1")
        late_codes = keep.tile([P, 2 * BANK], U32, name="late", align_bytes=64)
        for b in range(2):
            scales = kept([P, BANK], U8, "w3_%d1_sc" % b)
            codes = late_codes[:, BANK * b : BANK * (b + 1)]
            nc.vector.quantize_mx(codes.bitcast(FP8X4), scales[:], staged[5 + b][:])
            w3_mx[b, 1] = codes, scales

        for g in range(2):
            for t in range(PACK):
                acc = psum.tile([P, BANK], F32, name="pre")
                for b in range(2):
                    codes, scales = w3_mx[b, g]
                    nc.tensor.matmul_mx(
                        acc[:], lhsT=codes[:, P * t : P * (t + 1)].bitcast(FP8X4), lhsT_scale=scales[:, P * t : P * (t + 1)],
                        rhs=z_mx[b][0][:].bitcast(FP8X4), rhs_scale=z_mx[b][1][:],
                        start=(b == 0), stop=(b == 1),
                    )
                nc.scalar.copy(seam[PACK * g + t][:, :M], acc[:])
        for t in range(PACK):
            scale_own(PACK + t)

        y_sc = [kept([P, S], U8, "y_sc%d" % g) for g in range(2)]
        rounded = {}

        totals = {}

        def fetch(k, t):
            g, lo, width = CHUNKS[k]
            if t == 0:
                totals[k] = new_quad()
            n = PACK * g + t
            nc.vector.tensor_tensor(
                totals[k][:, t, :width], seam[n][:].indirect(p3[:, lo // 16 : (lo + width) // 16]),
                h[n][:, lo : lo + width], ALU.add,
            )

        def finish(k):
            g, lo, width = CHUNKS[k]
            total = totals[k]
            y = blend_raw[g, lo // BANK]
            cols = slice(lo % BANK, lo % BANK + width)
            nc.vector.tensor_tensor(y[:, :, cols], total[:, :, :width], y[:, :, cols], ALU.mult)
            rows = out_0[GROUP * g : GROUP * (g + 1), lo : lo + width]
            nc.sync.dma_start(rows.rearrange("(p t) j -> p t j", t=PACK), y[:, :, cols])
            stage = new_stage()
            if k == len(CHUNKS) - 1:
                nc.vector.tensor_copy(woven(stage, width), paired(y, lo % BANK, width))
            else:
                nc.scalar.copy(woven(stage, width), paired(y, lo % BANK, width))
            rounded[k] = stage

        def planes(k):
            g, lo, width = CHUNKS[k]
            codes = kept([P, width], U32, "y_codes%d" % k)
            nc.vector.quantize_mx(codes[:].bitcast(FP8X4), y_sc[g][:, lo : lo + width], rounded[k][:, : PACK * width])
            words = out_1[g].rearrange("p m t -> p (m t)")[:, PACK * lo : PACK * (lo + width)]
            nc.sync.dma_start(words.bitcast(I32), codes[:].bitcast(I32))
            if lo + width == S:
                for q in range(4):
                    queue = nc.scalar if g == 1 and q % 2 else nc.sync
                    queue.dma_start(
                        out_2[g, 4 * q : 4 * q + 4, :].bitcast(I32), y_sc[g][32 * q : 32 * q + 4, :].bitcast(I32)
                    )

        for k in range(len(CHUNKS)):
            fetch(k, 0)
            if k:
                finish(k - 1)
            for t in range(1, PACK):
                fetch(k, t)
            if k:
                planes(k - 1)
        finish(len(CHUNKS) - 1)
        planes(len(CHUNKS) - 1)
